import numpy as np
import ml_dtypes


def mxq(x, axis, fmt="e4m3"):
    dtype, down = {"e4m3": (ml_dtypes.float8_e4m3fn, 7), "e5m2": (ml_dtypes.float8_e5m2, 14)}[fmt]
    v = np.moveaxis(np.asarray(x, np.float32).astype(ml_dtypes.bfloat16).astype(np.float64), axis, -1)
    blocks = v.reshape(v.shape[:-1] + (-1, 32))
    amax = np.abs(blocks).max(-1, keepdims=True)
    byte = np.maximum(np.where(amax > 0, np.frexp(amax)[1] - 1 + 127, 0) - down, 1)
    scale = np.exp2(byte - 127.0)
    codes = (blocks / scale).astype(np.float32).astype(dtype).astype(np.float64)
    return np.moveaxis((codes * scale).reshape(v.shape), -1, axis)


WIDE = False


def mx_kscale(k):
    if not WIDE:
        return np.ones(k)
    levels = np.array([10, -10, 5, -5, 0])
    if k % 512:
        return np.exp2(np.random.permutation(np.resize(levels, k // 32))).repeat(32)
    a = np.empty((k // 512, 16))
    for p in range(k // 512):
        a[p, :8] = np.random.permutation(np.resize(levels, 8))
        for g in range(8):
            far = levels[np.abs(levels - a[p, g]) >= 10]
            a[p, g + 8] = far[np.random.randint(len(far))]
    return np.exp2(a.ravel()).repeat(32)


def f64(x):
    return np.asarray(x).astype(np.float64)


def striped(idx):
    return np.tile(idx.reshape(-1, 16).T, (8, 1)).astype(np.uint16)


def unstriped(offs):
    return offs[:16].T.reshape(-1).astype(np.int64)


E2M1 = np.array([0.0, 0.5, 1.0, 1.5, 2.0, 3.0, 4.0, 6.0, -0.0, -0.5, -1.0, -1.5, -2.0, -3.0, -4.0, -6.0])


def pack_weight(w, fmt):
    k, n = w.shape
    w = f64(np.asarray(w, np.float32).astype(ml_dtypes.bfloat16)).reshape(k // 32, 32, n)
    amax = np.abs(w).max(1)
    if fmt == "e4m3":
        byte = np.frexp(amax)[1] - 1 + 127 - 7
    else:
        mant, ex = np.frexp(amax / 6.0)
        byte = np.where(mant > 0.5, ex, ex - 1) + 127
    byte = np.clip(np.where(amax > 0, byte, 1), 1, 254)
    scaled = (w * np.exp2(127.0 - byte)[:, None, :]).reshape(k, n).astype(np.float32)
    by_word = np.ascontiguousarray(scaled.reshape(k // 512, 128, 4, n).transpose(0, 1, 3, 2))
    if fmt == "e4m3":
        words = by_word.astype(ml_dtypes.float8_e4m3fn).view(np.uint8)
    else:
        c = by_word.astype(ml_dtypes.float4_e2m1fn).view(np.uint8) & 0xF
        words = (c[..., 0::2] | (c[..., 1::2] << 4)).reshape(k // 512, 128, 2 * n)
    return np.ascontiguousarray(words), np.ascontiguousarray(byte.astype(np.uint8).reshape(k // 512, 16, n))


def unpack_weight(words, scales, fmt):
    g, _, n = scales.shape
    words = np.ascontiguousarray(words).reshape(g, 128, n, -1)
    if fmt == "e4m3":
        vals = words.view(ml_dtypes.float8_e4m3fn).astype(np.float64)
    else:
        nib = np.empty((g, 128, n, 4), np.uint8)
        nib[..., 0::2] = words & 0xF
        nib[..., 1::2] = words >> 4
        vals = E2M1[nib]
    vals = vals * np.repeat(np.exp2(scales.astype(np.float64) - 127.0), 8, axis=1)[..., None]
    return vals.transpose(0, 1, 3, 2).reshape(g * 512, n)


def gelu(v):
    return 0.5 * v * (1.0 + np.tanh(np.sqrt(2.0 / np.pi) * (v + 0.044715 * v**3)))


def striped8(idx):
    return np.concatenate([v.reshape(-1, 16).T for v in idx]).astype(np.uint16)


def unstriped8(offs):
    return np.stack([offs[16 * g:16 * g + 16].T.reshape(-1) for g in range(8)]).astype(np.int64)


def runs(v, idx8):
    k = np.arange(v.shape[0])
    return v[k[:, None], idx8[k % 512 // 64]]


K, K2, T, S, H, N = 1024, 512, 2048, 1024, 1024, 512

def setup_inputs():
    n = np.random.standard_normal
    s = mx_kscale(K)[:, None]
    s2 = mx_kscale(K2)[:, None]
    u = mx_kscale(H)[:, None]
    tab_words, tab_scales = pack_weight(n((K, T)) * s, "e4m3")
    tab2_words, tab2_scales = pack_weight(n((K2, T)) * s2, "e4m3")
    w2_words, w2_scales = pack_weight(n((K2, H)) / np.sqrt(K2) / s2 * u.T, "e2m1")
    wr_words, wr_scales = pack_weight(n((K, N)) / np.sqrt(K) / s, "e4m3")
    return {
        "tab_words": tab_words, "tab_scales": tab_scales,
        "tab2_words": tab2_words, "tab2_scales": tab2_scales,
        "offs": striped8(np.stack([np.random.permutation(T)[:S] for _ in range(8)])),
        "offs2": striped(np.random.permutation(T)[:S]),
        "w1": (n((K, H)) / np.sqrt(K) / s * u.T).astype(np.float32),
        "w2_words": w2_words, "w2_scales": w2_scales,
        "slack": ((0.5 + 0.3 * n(H)) * u[:, 0]).astype(np.float32),
        "low": ((-0.8 + 0.3 * n(H)) * u[:, 0]).astype(np.float32),
        "w3": (n((H, N)) / np.sqrt(H) / u).astype(np.float32),
        "wr_words": wr_words, "wr_scales": wr_scales,
        "trim": (0.5 * n(N)).astype(np.float32),
    }

def reference(tab_words, tab_scales, tab2_words, tab2_scales, offs, offs2, w1, w2_words, w2_scales,
              slack, low, w3, wr_words, wr_scales, trim):
    v = runs(unpack_weight(tab_words, tab_scales, "e4m3"), unstriped8(offs))
    v2 = unpack_weight(tab2_words, tab2_scales, "e4m3")[:, unstriped(offs2)]
    w2 = unpack_weight(w2_words, w2_scales, "e2m1")
    wr = unpack_weight(wr_words, wr_scales, "e4m3")
    a = mxq(f64(w1), 0, "e4m3").T @ v
    b = (w2.T @ v2) + f64(slack)[:, None]
    h = np.maximum(np.minimum(a, b), f64(low)[:, None])
    hq = mxq(h, 0, "e4m3")
    y = mxq(f64(w3), 0, "e4m3").T @ hq + wr.T @ v
    return y + f64(trim)[:, None]

@@ -1,0 +1,403 @@
+from contextlib import ExitStack
+
+import concourse.mybir as mybir
+from concourse.masks import make_identity
+
+K, K2, T, S, H, N = 1024, 512, 2048, 1024, 1024, 512
+FLOPS = 2 * S * (K * H + K2 * H + H * N + K * N)
+
+F32 = mybir.dt.float32
+BF16 = mybir.dt.bfloat16
+I32 = mybir.dt.int32
+U32 = mybir.dt.uint32
+U16 = mybir.dt.uint16
+U8 = mybir.dt.uint8
+FP8X4 = mybir.dt.float8_e4m3fn_x4
+FP4X4 = mybir.dt.float4_e2m1fn_x4
+ALU = mybir.AluOpType
+IDENT = mybir.ActivationFunctionType.Identity
+
+P = 128
+PASS = 512
+HALF = 512
+QUART = 256
+UNIT = 128
+
+
+def tile_list_hold_trim_features_kernel(
+    tc, tab_words, tab_scales, tab2_words, tab2_scales, offs, offs2, w1, w2_words, w2_scales,
+    slack, low, w3, wr_words, wr_scales, trim, out,
+):
+    nc = tc.nc
+    with ExitStack() as ctx:
+        keep = ctx.enter_context(tc.tile_pool(name="keep", bufs=1))
+        psum = ctx.enter_context(tc.psum_pool(name="psum", bufs=1))
+
+        def held(shape, dtype, name, tag=None):
+            return keep.tile(shape, dtype, name=name, tag=tag or name, align_bytes=64)
+
+        def by_vector(shape, dtype, name):
+            return keep.tile(shape, dtype, name=name, tag="by_vector", bufs=40, align_bytes=64)
+
+        def by_scalar(shape, dtype, name):
+            return keep.tile(shape, dtype, name=name, tag="by_scalar", bufs=7, align_bytes=64)
+
+        def by_vector_wide(shape, dtype, name):
+            return held(shape, dtype, name)
+
+        offs_t = held([P, S // 16], U16, "offs_t")
+        offs2_t = held([P, S // 16], U16, "offs2_t")
+        sc_win = held([P, T], U8, "sc_win")
+        sc2_win = held([P, T], U8, "sc2_win")
+        w2s_raw = held([P, H], U8, "w2s_raw")
+        w2_raw = held([P, 2 * H], U8, "w2_raw")
+        wr = held([P, 2, N], U32, "wr")
+        wrs = held([P, 2, N], U8, "wrs")
+        rows = held([P, 2 * P], F32, "rows")
+        ident = held([P, P], F32, "ident")
+        trim_t = held([P, 4], F32, "trim_t")
+        low_pat = held([P, 2, UNIT], BF16, "low_pat")
+        win, w1raw, w3raw, w1q, w3q, v, v2, allow, least, clipped, hq, ybank, one = ({} for i in range(13))
+
+        def clear(eng, tile):
+            eng.memset(tile.bitcast(I32), 0)
+
+        def load_sc():
+            src = tab_scales.rearrange("a (g e) t -> e g a t", e=2)
+            for e in range(2):
+                nc.sync.dma_start(sc_win[e:P:8, :].bitcast(I32), src[e].bitcast(I32))
+
+        def load_plane(dst, src, queue=nc.sync, quads=(0, 1, 2, 3)):
+            for d in quads:
+                queue.dma_start(dst[32 * d : 32 * d + 4, :].bitcast(I32), src[4 * d : 4 * d + 4, :].bitcast(I32))
+
+        def load_wrs():
+            for d in range(4):
+                nc.sync.dma_start(
+                    wrs[32 * d : 32 * d + 4, :, :].bitcast(I32),
+                    wr_scales[:, 4 * d : 4 * d + 4, :].rearrange("a r n -> r a n").bitcast(I32),
+                )
+
+        def load_wr():
+            nc.sync.dma_start(wr[:].bitcast(I32), wr_words.rearrange("a p n i -> p a (n i)").bitcast(I32))
+
+        def load_w2():
+            nc.sync.dma_start(w2_raw[:].bitcast(I32), w2_words[0].bitcast(I32))
+
+        def load_words(src, name):
+            win[name] = held([P, T], U32, name)
+            nc.sync.dma_start(win[name][:].bitcast(I32), src.rearrange("p t i -> p (t i)").bitcast(I32))
+
+        def load_w1(a, g):
+            w1raw[a, g] = held([P, 4, PASS], F32, "w1raw%d%d" % (a, g))
+            src = w1[PASS * a : PASS * (a + 1), PASS * g : PASS * (g + 1)]
+            nc.sync.dma_start(w1raw[a, g][:], src.rearrange("(p j) c -> p j c", j=4))
+
+        def load_w3(g, tag):
+            w3raw[g] = held([P, 4, N], F32, "w3raw%d" % g, tag)
+            src = w3[PASS * g : PASS * (g + 1), :].rearrange("(b t i) n -> t b i n", t=4, i=8)
+            for t in range(4):
+                nc.sync.dma_start(w3raw[g][:, t, :], src[t])
+
+        def load_rows():
+            for r, vec in ((0, slack), (4, low)):
+                nc.scalar.dma_start(
+                    rows[r : r + 4, :].rearrange("t (b i) -> t b i", i=8),
+                    vec.rearrange("(b t i) -> t b i", t=4, i=8),
+                )
+
+        def load_trim():
+            with nc.allow_non_contiguous_dma(reason="one value of trim for each partition"):
+                nc.sync.dma_start(trim_t[:], trim.rearrange("(q p) -> p q", p=P))
+
+        def turn_rows():
+            turned = psum.tile([P, 4, P], F32, name="turned", tag="y", bufs=6)
+            for g in range(2):
+                nc.tensor.transpose(turned[:, g, :], rows[:, P * g : P * (g + 1)], ident[:])
+            one["consts"] = held([P, 2, 8], F32, "consts", "w1raw00")
+            nc.scalar.copy(one["consts"][:], turned[:, 0:2, 0:8])
+            for g in range(2):
+                nc.scalar.copy(
+                    low_pat[:, g, :].rearrange("p (n t) -> p n t", t=4),
+                    one["consts"][:, g, 4:8].unsqueeze(1).to_broadcast([P, UNIT // 4, 4]),
+                )
+
+        def gather_sc():
+            one["sc_got"] = by_vector([P, S], U8, "sc_got")
+            nc.vector.tensor_copy(one["sc_got"][:], sc_win[:].indirect(offs_t[:]))
+
+        def copy_sc():
+            one["v_sc"] = held([P, S], U8, "v_sc")
+            nc.vector.tensor_copy(one["v_sc"][:].bitcast(I32), one["sc_got"][:].bitcast(I32))
+
+        def move_sc():
+            for a in range(2):
+                for e in range(2):
+                    nc.sync.dma_start(
+                        one["v_sc"][8 * a + 2 + e : P : 32, :].bitcast(I32),
+                        one["sc_got"][16 + 8 * a + e : P : 32, :].bitcast(I32),
+                    )
+
+        def gather_sc2():
+            one["v2_sc"] = by_vector([P, S], U8, "v2_sc")
+            nc.vector.tensor_copy(one["v2_sc"][:], sc2_win[:].indirect(offs2_t[:]))
+
+        def gather_words(name, lst, h):
+            got = by_vector([P, HALF], U32, "got_%s_%d" % (name, h))
+            cols = slice(HALF // 16 * h, HALF // 16 * (h + 1))
+            nc.vector.tensor_copy(got[:], win[name][:].indirect(lst[:, cols]))
+            return got
+
+        def gather_v(a, h):
+            v[a, h] = gather_words("tab%d" % a, offs_t, h)
+
+        def gather_v2(h):
+            v2[h] = gather_words("tab2", offs2_t, h)
+
+        def order_w2():
+            one["w2"] = by_vector([P, 2 * H], U8, "w2")
+            nc.vector.tensor_copy(
+                one["w2"][:].bitcast(I32).rearrange("p (g t b q) -> p g t b q", g=2, t=4, q=4),
+                w2_raw[:].bitcast(I32).rearrange("p (g b t q) -> p g t b q", g=2, t=4, q=4),
+            )
+            one["w2s"] = by_vector([P, H], U8, "w2s")
+            nc.vector.tensor_copy(
+                one["w2s"][:].bitcast(I32).rearrange("p (g t b q) -> p g t b q", g=2, t=4, q=2),
+                w2s_raw[:].bitcast(I32).rearrange("p (g b t q) -> p g t b q", g=2, t=4, q=2),
+            )
+
+        def quantise(values, width, name):
+            codes = by_vector([P, width], U32, name + "_c")
+            scales = held([P, width], U8, name + "_s")
+            nc.vector.quantize_mx(out=codes[:].bitcast(FP8X4), scales=scales[:], in_=values)
+            return codes, scales
+
+        def cast_w1(a, g, on_vector=False):
+            make, move = (by_vector_wide, nc.vector.tensor_copy) if on_vector else (by_scalar, nc.scalar.copy)
+            grouped = make([P, 4, P, 4], BF16, "w1g%d%d" % (a, g))
+            src = w1raw[a, g][:].rearrange("p j (b t h i) -> p t b h j i", t=4, h=2, i=4)
+            for t in range(4):
+                move(grouped[:, t, :, :].rearrange("p (b h i) j -> p b h j i", h=2, i=4), src[:, t])
+            one["w1g", a, g] = grouped
+
+        def quant_w1(a, g):
+            w1q[a, g] = quantise(one["w1g", a, g][:].rearrange("p t m j -> p (t m j)"), PASS, "w1q%d%d" % (a, g))
+
+        def cast_w3(g):
+            grouped = by_scalar([P, N, 4], BF16, "w3g%d" % g)
+            nc.scalar.copy(
+                grouped[:].rearrange("p (c i) t -> p c t i", i=4),
+                w3raw[g][:].rearrange("p t (c i) -> p c t i", i=4),
+            )
+            one["w3g", g] = grouped
+
+        def quant_w3(g):
+            w3q[g] = quantise(one["w3g", g][:].rearrange("p n t -> p (n t)"), N, "w3q%d" % g)
+
+        def booked(h, g):
+            allow[h, g] = by_scalar([P, 4, HALF], F32, "allow%d%d" % (h, g))
+            for t in range(4):
+                bank = psum.tile([P, HALF], F32, name="b%d%d" % (h, g), tag="y", bufs=6)
+                c0 = PASS * g + P * t
+                nc.tensor.matmul_mx(
+                    out=bank[:],
+                    lhsT=one["w2"][:, 2 * c0 : 2 * (c0 + P)].bitcast(FP4X4),
+                    lhsT_scale=one["w2s"][:, c0 : c0 + P],
+                    rhs=v2[h][:].bitcast(FP8X4),
+                    rhs_scale=one["v2_sc"][:, HALF * h : HALF * (h + 1)],
+                    start=True,
+                    stop=True,
+                )
+                nc.scalar.activation(allow[h, g][:, t, :], bank[:], IDENT, bias=one["consts"][:, g, t : t + 1])
+
+        def unit(jq, g, u):
+            h, j0 = divmod(QUART * jq, HALF)
+            least[jq, g, u] = by_vector([P, 4 * UNIT], BF16, "least%d%d" % (jq, g))
+            bank = psum.tile([P, 4 * UNIT], F32, name="a%d%d" % (jq, g), tag="a", bufs=2)
+            c0 = j0 + UNIT * u
+            for t in range(4):
+                for a in (1, 0):
+                    codes, scales = w1q[a, g]
+                    nc.tensor.matmul_mx(
+                        out=bank[:, UNIT * t : UNIT * (t + 1)],
+                        lhsT=codes[:, P * t : P * (t + 1)].bitcast(FP8X4),
+                        lhsT_scale=scales[:, P * t : P * (t + 1)],
+                        rhs=v[a, h][:, c0 : c0 + UNIT].bitcast(FP8X4),
+                        rhs_scale=one["v_sc"][8 * a : P, HALF * h + c0 : HALF * h + c0 + UNIT],
+                        start=(a == 1),
+                        stop=(a == 0),
+                    )
+            nc.vector.tensor_tensor(
+                least[jq, g, u][:].rearrange("p (c i t) -> p c t i", i=4, t=4),
+                bank[:].rearrange("p (t c i) -> p c t i", t=4, i=4),
+                allow[h, g][:, :, c0 : c0 + UNIT].rearrange("p t (c i) -> p c t i", i=4),
+                ALU.min,
+            )
+
+        def clip(jq, g, u):
+            if u == 0:
+                clipped[jq, g] = by_vector([P, 4 * QUART], BF16, "clip%d%d" % (jq, g))
+            nc.vector.tensor_tensor(
+                clipped[jq, g][:, 4 * UNIT * u : 4 * UNIT * (u + 1)].rearrange("p (k x) -> p k x", x=UNIT),
+                least[jq, g, u][:].rearrange("p (k x) -> p k x", x=UNIT),
+                low_pat[:, g, :].unsqueeze(1).to_broadcast([P, 4, UNIT]),
+                ALU.max,
+            )
+
+        def quant_h(jq, g):
+            hq[jq, g] = quantise(clipped[jq, g][:], QUART, "hq%d%d" % (jq, g))
+
+        def y_pass(jq, step, tag="y", bufs=6):
+            h, j0 = divmod(QUART * jq, HALF)
+            for k in range(2):
+                first = (jq, k) not in ybank
+                if first:
+                    ybank[jq, k] = psum.tile([P, 2, QUART], F32, name="y%d%d" % (jq, k), tag=tag, bufs=bufs)
+                for s in range(2):
+                    q = 2 * k + s
+                    cols = slice(P * q, P * (q + 1))
+                    if step < 2:
+                        lhs, lhs_s = wr[:, step, cols], wrs[:, step, cols]
+                        rhs = v[step, h][:, j0 : j0 + QUART]
+                        rhs_s = one["v_sc"][8 * step : P, QUART * jq : QUART * (jq + 1)]
+                    else:
+                        lhs, lhs_s = w3q[step - 2][0][:, cols], w3q[step - 2][1][:, cols]
+                        rhs, rhs_s = hq[jq, step - 2][0][:], hq[jq, step - 2][1][:]
+                    nc.tensor.matmul_mx(
+                        out=ybank[jq, k][:, s, :],
+                        lhsT=lhs.bitcast(FP8X4),
+                        lhsT_scale=lhs_s,
+                        rhs=rhs.bitcast(FP8X4),
+                        rhs_scale=rhs_s,
+                        start=(first and s == 0),
+                        stop=(step == 3 and s == 1),
+                    )
+
+        def y_out(jq, k, on_vector=False):
+            res = keep.tile([P, 2, QUART], F32, name="res%d%d" % (jq, k), tag="res", bufs=5, align_bytes=64)
+            for s in range(2):
+                bias = trim_t[:, 2 * k + s : 2 * k + s + 1]
+                if on_vector:
+                    nc.vector.tensor_scalar(res[:, s, :], ybank[jq, k][:, s, :], bias, None, ALU.add)
+                else:
+                    nc.scalar.activation(res[:, s, :], ybank[jq, k][:, s, :], IDENT, bias=bias)
+            dst = out[2 * P * k : 2 * P * (k + 1), QUART * jq : QUART * (jq + 1)]
+            nc.sync.dma_start(dst.rearrange("(s p) n -> p s n", p=P), res[:])
+
+        clear(nc.gpsimd, sc_win[:])
+        nc.vector.memset(rows[:], 0.0)
+        clear(nc.vector, sc2_win[:])
+        clear(nc.vector, w2s_raw[:])
+        clear(nc.vector, wrs[:].rearrange("p a n -> p (a n)"))
+        load_rows()
+        make_identity(nc, ident[:])
+        nc.sync.dma_start(offs_t[:], offs)
+        load_sc()
+        nc.sync.dma_start(offs2_t[:], offs2)
+        load_w1(0, 0)
+        load_plane(sc2_win, tab2_scales[0])
+        load_words(tab2_words[0], "tab2")
+        load_w2()
+        load_plane(w2s_raw, w2_scales[0])
+        load_w1(1, 0)
+        load_words(tab_words[0], "tab0")
+        gather_sc()
+        copy_sc()
+        move_sc()
+        load_words(tab_words[1], "tab1")
+        load_wr()
+        load_wrs()
+        load_w3(0, "tab2")
+        load_w1(0, 1)
+        load_w1(1, 1)
+        load_w3(1, "tab0")
+        load_trim()
+        gather_sc2()
+        gather_v2(0)
+        order_w2()
+        cast_w1(0, 0)
+        turn_rows()
+        booked(0, 0)
+        gather_v2(1)
+        booked(1, 0)
+        cast_w1(1, 0, True)
+        quant_w1(0, 0)
+        quant_w1(1, 0)
+        booked(0, 1)
+        booked(1, 1)
+        gather_v(0, 0)
+        gather_v(0, 1)
+        gather_v(1, 0)
+        gather_v(1, 1)
+        cast_w3(0)
+        cast_w1(0, 1)
+        cast_w1(1, 1)
+        cast_w3(1)
+        unit(0, 0, 0)
+        unit(0, 0, 1)
+        clip(0, 0, 0)
+        unit(1, 0, 0)
+        clip(0,0, 1)
+        unit(1, 0, 1)
+        quant_h(0,0)
+        clip(1, 0, 0)
+        quant_w3(0)
+        unit(2, 0, 0)
+        clip(1,0, 1)
+        y_pass(0, 0)
+        y_pass(0, 1)
+        unit(2, 0, 1)
+        quant_h(1,0)
+        clip(2, 0, 0)
+        quant_w1(0, 1)
+        y_pass(0, 2)
+        y_pass(1, 0)
+        unit(3, 0, 0)
+        clip(2,0, 1)
+        quant_w1(1, 1)
+        y_pass(1, 1)
+        y_pass(1, 2)
+        unit(3, 0, 1)
+        quant_h(2,0)
+        clip(3, 0, 0)
+        unit(0, 1, 0)
+        clip(3,0, 1)
+        quant_w3(1)
+        unit(0, 1, 1)
+        quant_h(3,0)
+        clip(0, 1, 0)
+        y_pass(2, 2)
+        y_pass(2, 0)
+        y_pass(2, 1)
+        unit(1, 1, 0)
+        clip(0,1, 1)
+        unit(1, 1, 1)
+        quant_h(0,1)
+        clip(1, 1, 0)
+        y_pass(0, 3)
+        y_out(0, 0)
+        y_out(0, 1)
+        unit(2, 1, 0)
+        clip(1,1, 1)
+        unit(2, 1, 1)
+        quant_h(1,1)
+        clip(2, 1, 0)
+        y_pass(1, 3)
+        y_out(1, 0)
+        y_out(1, 1)
+        unit(3, 1, 0)
+        clip(2,1, 1)
+        unit(3, 1, 1)
+        quant_h(2,1)
+        clip(3, 1, 0)
+        y_pass(2, 3)
+        y_out(2, 0)
+        y_out(2, 1)
+        y_pass(3, 0)
+        y_pass(3, 1)
+        y_pass(3, 2)
+        clip(3,1, 1)
+        quant_h(3,1)
+        y_pass(3, 3)
+        y_out(3, 0)
+        y_out(3, 1, True)

@@ -175,9 +175,9 @@ def tile_list_hold_trim_features_kernel(
         def cast_w1(a, g, on_vector=False):
             make, move = (by_vector_wide, nc.vector.tensor_copy) if on_vector else (by_scalar, nc.scalar.copy)
             grouped = make([P, 4, P, 4], BF16, "w1g%d%d" % (a, g))
-            src = w1raw[a, g][:].rearrange("p j (b t h i) -> p t b h j i", t=4, h=2, i=4)
+            src = w1raw[a, g][:].rearrange("p j (b t h i) -> p t b h j i", t=4, h=4, i=2)
             for t in range(4):
-                move(grouped[:, t, :, :].rearrange("p (b h i) j -> p b h j i", h=2, i=4), src[:, t])
+                move(grouped[:, t, :, :].rearrange("p (b h i) j -> p b h j i", h=4, i=2), src[:, t])
             one["w1g", a, g] = grouped
 
         def quant_w1(a, g):
@@ -186,8 +186,8 @@ def tile_list_hold_trim_features_kernel(
         def cast_w3(g):
             grouped = by_scalar([P, N, 4], BF16, "w3g%d" % g)
             nc.scalar.copy(
-                grouped[:].rearrange("p (c i) t -> p c t i", i=4),
-                w3raw[g][:].rearrange("p t (c i) -> p c t i", i=4),
+                grouped[:].rearrange("p (c i) t -> p c t i", i=2),
+                w3raw[g][:].rearrange("p t (c i) -> p c t i", i=2),
             )
             one["w3g", g] = grouped
 
@@ -228,9 +228,9 @@ def tile_list_hold_trim_features_kernel(
                         stop=(a == 0),
                     )
             nc.vector.tensor_tensor(
-                least[jq, g, u][:].rearrange("p (c i t) -> p c t i", i=4, t=4),
-                bank[:].rearrange("p (t c i) -> p c t i", t=4, i=4),
-                allow[h, g][:, :, c0 : c0 + UNIT].rearrange("p t (c i) -> p c t i", i=4),
+                least[jq, g, u][:].rearrange("p (c i t) -> p c t i", i=2, t=4),
+                bank[:].rearrange("p (t c i) -> p c t i", t=4, i=2),
+                allow[h, g][:, :, c0 : c0 + UNIT].rearrange("p t (c i) -> p c t i", i=2),
                 ALU.min,
             )
 

@@ -37,7 +37,7 @@ def tile_list_hold_trim_features_kernel(
             return keep.tile(shape, dtype, name=name, tag=tag or name, align_bytes=64)
 
         def by_vector(shape, dtype, name):
-            return keep.tile(shape, dtype, name=name, tag="by_vector", bufs=40, align_bytes=64)
+            return keep.tile(shape, dtype, name=name, tag="by_vector", bufs=42, align_bytes=64)
 
         def by_scalar(shape, dtype, name):
             return keep.tile(shape, dtype, name=name, tag="by_scalar", bufs=7, align_bytes=64)
@@ -68,14 +68,14 @@ def tile_list_hold_trim_features_kernel(
                 nc.sync.dma_start(sc_win[e:P:8, :].bitcast(I32), src[e].bitcast(I32))
 
         def load_plane(dst, src, queue=nc.sync, quads=(0, 1, 2, 3)):
-            for d in quads:
-                queue.dma_start(dst[32 * d : 32 * d + 4, :].bitcast(I32), src[4 * d : 4 * d + 4, :].bitcast(I32))
+            for r in range(4):
+                queue.dma_start(dst[r:P:32, :].bitcast(I32), src[r:16:4, :].bitcast(I32))
 
         def load_wrs():
-            for d in range(4):
+            for r in range(4):
                 nc.sync.dma_start(
-                    wrs[32 * d : 32 * d + 4, :, :].bitcast(I32),
-                    wr_scales[:, 4 * d : 4 * d + 4, :].rearrange("a r n -> r a n").bitcast(I32),
+                    wrs[r:P:32, :, :].bitcast(I32),
+                    wr_scales[:, r:16:4, :].rearrange("a r n -> r a n").bitcast(I32),
                 )
 
         def load_wr():
@@ -111,7 +111,7 @@ def tile_list_hold_trim_features_kernel(
                 nc.sync.dma_start(trim_t[:], trim.rearrange("(q p) -> p q", p=P))
 
         def turn_rows():
-            turned = psum.tile([P, 4, P], F32, name="turned", tag="y", bufs=6)
+            turned = psum.tile([P, 4, P], F32, name="turned", tag="y", bufs=5)
             for g in range(2):
                 nc.tensor.transpose(turned[:, g, :], rows[:, P * g : P * (g + 1)], ident[:])
             one["consts"] = held([P, 2, 8], F32, "consts", "w1raw00")
@@ -197,7 +197,7 @@ def tile_list_hold_trim_features_kernel(
         def booked(h, g):
             allow[h, g] = by_scalar([P, 4, HALF], F32, "allow%d%d" % (h, g))
             for t in range(4):
-                bank = psum.tile([P, HALF], F32, name="b%d%d" % (h, g), tag="y", bufs=6)
+                bank = psum.tile([P, HALF], F32, name="b%d%d" % (h, g), tag="y", bufs=5)
                 c0 = PASS * g + P * t
                 nc.tensor.matmul_mx(
                     out=bank[:],
@@ -213,7 +213,7 @@ def tile_list_hold_trim_features_kernel(
         def unit(jq, g, u):
             h, j0 = divmod(QUART * jq, HALF)
             least[jq, g, u] = by_vector([P, 4 * UNIT], BF16, "least%d%d" % (jq, g))
-            bank = psum.tile([P, 4 * UNIT], F32, name="a%d%d" % (jq, g), tag="a", bufs=2)
+            bank = psum.tile([P, 4 * UNIT], F32, name="a%d%d" % (jq, g), tag="a", bufs=3)
             c0 = j0 + UNIT * u
             for t in range(4):
                 for a in (1, 0):
@@ -247,11 +247,12 @@ def tile_list_hold_trim_features_kernel(
         def quant_h(jq, g):
             hq[jq, g] = quantise(clipped[jq, g][:], QUART, "hq%d%d" % (jq, g))
 
-        def y_pass(jq, step, tag="y", bufs=6):
+        def y_pass(jq, step, tag="y", bufs=5):
             h, j0 = divmod(QUART * jq, HALF)
             for k in range(2):
                 first = (jq, k) not in ybank
                 if first:
+                    tag, bufs = ("a", 3) if (jq, k) == (3, 1) else (tag, bufs)
                     ybank[jq, k] = psum.tile([P, 2, QUART], F32, name="y%d%d" % (jq, k), tag=tag, bufs=bufs)
                 for s in range(2):
                     q = 2 * k + s
@@ -274,7 +275,10 @@ def tile_list_hold_trim_features_kernel(
                     )
 
         def y_out(jq, k, on_vector=False):
-            res = keep.tile([P, 2, QUART], F32, name="res%d%d" % (jq, k), tag="res", bufs=5, align_bytes=64)
+            if on_vector:
+                res = by_vector([P, 2, QUART], F32, "res%d%d" % (jq, k))
+            else:
+                res = keep.tile([P, 2, QUART], F32, name="res%d%d" % (jq, k), tag="res", bufs=4, align_bytes=64)
             for s in range(2):
                 bias = trim_t[:, 2 * k + s : 2 * k + s + 1]
                 if on_vector:
@@ -305,11 +309,11 @@ def tile_list_hold_trim_features_kernel(
         copy_sc()
         move_sc()
         load_words(tab_words[1], "tab1")
+        load_w1(0, 1)
+        load_w1(1, 1)
         load_wr()
         load_wrs()
         load_w3(0, "tab2")
-        load_w1(0, 1)
-        load_w1(1, 1)
         load_w3(1, "tab0")
         load_trim()
         gather_sc2()
@@ -329,9 +333,9 @@ def tile_list_hold_trim_features_kernel(
         gather_v(0, 1)
         gather_v(1, 0)
         gather_v(1, 1)
-        cast_w3(0)
         cast_w1(0, 1)
         cast_w1(1, 1)
+        cast_w3(0)
         cast_w3(1)
         unit(0, 0, 0)
         unit(0, 0, 1)
@@ -341,42 +345,42 @@ def tile_list_hold_trim_features_kernel(
         unit(1, 0, 1)
         quant_h(0,0)
         clip(1, 0, 0)
-        quant_w3(0)
         unit(2, 0, 0)
         clip(1,0, 1)
-        y_pass(0, 0)
-        y_pass(0, 1)
         unit(2, 0, 1)
         quant_h(1,0)
         clip(2, 0, 0)
         quant_w1(0, 1)
-        y_pass(0, 2)
-        y_pass(1, 0)
         unit(3, 0, 0)
         clip(2,0, 1)
         quant_w1(1, 1)
-        y_pass(1, 1)
-        y_pass(1, 2)
         unit(3, 0, 1)
         quant_h(2,0)
         clip(3, 0, 0)
+        y_pass(0, 0)
+        y_pass(0, 1)
+        y_pass(1, 0)
+        y_pass(1, 1)
         unit(0, 1, 0)
         clip(3,0, 1)
-        quant_w3(1)
+        quant_w3(0)
         unit(0, 1, 1)
         quant_h(3,0)
         clip(0, 1, 0)
-        y_pass(2, 2)
         y_pass(2, 0)
         y_pass(2, 1)
+        y_pass(0, 2)
+        y_pass(1, 2)
         unit(1, 1, 0)
         clip(0,1, 1)
+        quant_w3(1)
         unit(1, 1, 1)
         quant_h(0,1)
         clip(1, 1, 0)
         y_pass(0, 3)
         y_out(0, 0)
         y_out(0, 1)
+        y_pass(2, 2)
         unit(2, 1, 0)
         clip(1,1, 1)
         unit(2, 1, 1)
@@ -386,18 +390,18 @@ def tile_list_hold_trim_features_kernel(
         y_out(1, 0)
         y_out(1, 1)
         unit(3, 1, 0)
-        clip(2,1, 1)
-        unit(3, 1, 1)
-        quant_h(2,1)
+        clip(2, 1, 1)
         clip(3, 1, 0)
+        quant_h(2, 1)
+        unit(3, 1, 1)
         y_pass(2, 3)
-        y_out(2, 0)
-        y_out(2, 1)
         y_pass(3, 0)
         y_pass(3, 1)
         y_pass(3, 2)
-        clip(3,1, 1)
-        quant_h(3,1)
+        y_out(2, 0)
+        clip(3, 1, 1)
+        quant_h(3, 1)
+        y_out(2, 1, True)
         y_pass(3, 3)
         y_out(3, 0)
         y_out(3, 1, True)

@@ -37,7 +37,7 @@ def tile_list_hold_trim_features_kernel(
             return keep.tile(shape, dtype, name=name, tag=tag or name, align_bytes=64)
 
         def by_vector(shape, dtype, name):
-            return keep.tile(shape, dtype, name=name, tag="by_vector", bufs=42, align_bytes=64)
+            return keep.tile(shape, dtype, name=name, tag="by_vector", bufs=34, align_bytes=64)
 
         def by_scalar(shape, dtype, name):
             return keep.tile(shape, dtype, name=name, tag="by_scalar", bufs=7, align_bytes=64)
@@ -56,7 +56,7 @@ def tile_list_hold_trim_features_kernel(
         rows = held([P, 2 * P], F32, "rows")
         ident = held([P, P], F32, "ident")
         trim_t = held([P, 4], F32, "trim_t")
-        low_pat = held([P, 2, UNIT], BF16, "low_pat")
+        low_pat = held([P, 2, 4 * QUART], BF16, "low_pat")
         win, w1raw, w3raw, w1q, w3q, v, v2, allow, least, clipped, hq, ybank, one = ({} for i in range(13))
 
         def clear(eng, tile):
@@ -119,7 +119,7 @@ def tile_list_hold_trim_features_kernel(
             for g in range(2):
                 nc.scalar.copy(
                     low_pat[:, g, :].rearrange("p (n t) -> p n t", t=4),
-                    one["consts"][:, g, 4:8].unsqueeze(1).to_broadcast([P, UNIT // 4, 4]),
+                    one["consts"][:, g, 4:8].unsqueeze(1).to_broadcast([P, QUART, 4]),
                 )
 
         def gather_sc():
@@ -212,35 +212,35 @@ def tile_list_hold_trim_features_kernel(
 
         def unit(jq, g, u):
             h, j0 = divmod(QUART * jq, HALF)
-            least[jq, g, u] = by_vector([P, 4 * UNIT], BF16, "least%d%d" % (jq, g))
-            bank = psum.tile([P, 4 * UNIT], F32, name="a%d%d" % (jq, g), tag="a", bufs=3)
-            c0 = j0 + UNIT * u
-            for t in range(4):
+            if u == 0:
+                least[jq, g] = by_vector([P, 2, QUART, 2], BF16, "least%d%d" % (jq, g))
+            bank = psum.tile([P, 2, QUART], F32, name="a%d%d" % (jq, g), tag="a", bufs=3)
+            for e in range(2):
+                t = 2 * u + e
                 for a in (1, 0):
                     codes, scales = w1q[a, g]
                     nc.tensor.matmul_mx(
-                        out=bank[:, UNIT * t : UNIT * (t + 1)],
+                        out=bank[:, e, :],
                         lhsT=codes[:, P * t : P * (t + 1)].bitcast(FP8X4),
                         lhsT_scale=scales[:, P * t : P * (t + 1)],
-                        rhs=v[a, h][:, c0 : c0 + UNIT].bitcast(FP8X4),
-                        rhs_scale=one["v_sc"][8 * a : P, HALF * h + c0 : HALF * h + c0 + UNIT],
+                        rhs=v[a, h][:, j0 : j0 + QUART].bitcast(FP8X4),
+                        rhs_scale=one["v_sc"][8 * a : P, QUART * jq : QUART * (jq + 1)],
                         start=(a == 1),
                         stop=(a == 0),
                     )
             nc.vector.tensor_tensor(
-                least[jq, g, u][:].rearrange("p (c i t) -> p c t i", i=2, t=4),
-                bank[:].rearrange("p (t c i) -> p c t i", t=4, i=2),
-                allow[h, g][:, :, c0 : c0 + UNIT].rearrange("p t (c i) -> p c t i", i=2),
+                least[jq, g][:, u, :, :].rearrange("p (c i) e -> p c e i", i=4),
+                bank[:].rearrange("p e (c i) -> p c e i", i=4),
+                allow[h, g][:, 2 * u : 2 * u + 2, j0 : j0 + QUART].rearrange("p e (c i) -> p c e i", i=4),
                 ALU.min,
             )
 
-        def clip(jq, g, u):
-            if u == 0:
-                clipped[jq, g] = by_vector([P, 4 * QUART], BF16, "clip%d%d" % (jq, g))
+        def clip(jq, g):
+            clipped[jq, g] = by_vector([P, 4 * QUART], BF16, "clip%d%d" % (jq, g))
             nc.vector.tensor_tensor(
-                clipped[jq, g][:, 4 * UNIT * u : 4 * UNIT * (u + 1)].rearrange("p (k x) -> p k x", x=UNIT),
-                least[jq, g, u][:].rearrange("p (k x) -> p k x", x=UNIT),
-                low_pat[:, g, :].unsqueeze(1).to_broadcast([P, 4, UNIT]),
+                clipped[jq, g][:].rearrange("p (n u e) -> p n u e", u=2, e=2),
+                least[jq, g][:].rearrange("p u n e -> p n u e"),
+                low_pat[:, g, :].rearrange("p (n u e) -> p n u e", u=2, e=2),
                 ALU.max,
             )
 
@@ -310,9 +310,9 @@ def tile_list_hold_trim_features_kernel(
         move_sc()
         load_words(tab_words[1], "tab1")
         load_w1(0, 1)
-        load_w1(1, 1)
         load_wr()
         load_wrs()
+        load_w1(1, 1)
         load_w3(0, "tab2")
         load_w3(1, "tab0")
         load_trim()
@@ -339,68 +339,60 @@ def tile_list_hold_trim_features_kernel(
         cast_w3(1)
         unit(0, 0, 0)
         unit(0, 0, 1)
-        clip(0, 0, 0)
         unit(1, 0, 0)
-        clip(0,0, 1)
+        clip(0,0)
         unit(1, 0, 1)
         quant_h(0,0)
-        clip(1, 0, 0)
         unit(2, 0, 0)
-        clip(1,0, 1)
+        clip(1,0)
         unit(2, 0, 1)
         quant_h(1,0)
-        clip(2, 0, 0)
         quant_w1(0, 1)
         unit(3, 0, 0)
-        clip(2,0, 1)
+        clip(2,0)
         quant_w1(1, 1)
         unit(3, 0, 1)
         quant_h(2,0)
-        clip(3, 0, 0)
         y_pass(0, 0)
         y_pass(0, 1)
         y_pass(1, 0)
         y_pass(1, 1)
+        clip(3,0)
         unit(0, 1, 0)
-        clip(3,0, 1)
+        quant_h(3,0)
         quant_w3(0)
         unit(0, 1, 1)
-        quant_h(3,0)
-        clip(0, 1, 0)
         y_pass(2, 0)
         y_pass(2, 1)
         y_pass(0, 2)
         y_pass(1, 2)
         unit(1, 1, 0)
-        clip(0,1, 1)
+        clip(0,1)
         quant_w3(1)
         unit(1, 1, 1)
         quant_h(0,1)
-        clip(1, 1, 0)
         y_pass(0, 3)
         y_out(0, 0)
         y_out(0, 1)
         y_pass(2, 2)
         unit(2, 1, 0)
-        clip(1,1, 1)
+        clip(1,1)
         unit(2, 1, 1)
         quant_h(1,1)
-        clip(2, 1, 0)
         y_pass(1, 3)
         y_out(1, 0)
         y_out(1, 1)
         unit(3, 1, 0)
-        clip(2, 1, 1)
-        clip(3, 1, 0)
-        quant_h(2, 1)
+        clip(2,1)
         unit(3, 1, 1)
+        quant_h(2,1)
         y_pass(2, 3)
         y_pass(3, 0)
         y_pass(3, 1)
         y_pass(3, 2)
         y_out(2, 0)
-        clip(3, 1, 1)
-        quant_h(3, 1)
+        clip(3,1)
+        quant_h(3,1)
         y_out(2, 1, True)
         y_pass(3, 3)
         y_out(3, 0)

from contextlib import ExitStack

import concourse.mybir as mybir
from concourse.masks import make_identity

K, K2, T, S, H, N = 1024, 512, 2048, 1024, 1024, 512
FLOPS = 2 * S * (K * H + K2 * H + H * N + K * N)

F32 = mybir.dt.float32
BF16 = mybir.dt.bfloat16
I32 = mybir.dt.int32
U32 = mybir.dt.uint32
U16 = mybir.dt.uint16
U8 = mybir.dt.uint8
FP8X4 = mybir.dt.float8_e4m3fn_x4
FP4X4 = mybir.dt.float4_e2m1fn_x4
ALU = mybir.AluOpType
IDENT = mybir.ActivationFunctionType.Identity

P = 128
PASS = 512
HALF = 512
QUART = 256
UNIT = 128


def tile_list_hold_trim_features_kernel(
    tc, tab_words, tab_scales, tab2_words, tab2_scales, offs, offs2, w1, w2_words, w2_scales,
    slack, low, w3, wr_words, wr_scales, trim, out,
):
    nc = tc.nc
    with ExitStack() as ctx:
        keep = ctx.enter_context(tc.tile_pool(name="keep", bufs=1))
        psum = ctx.enter_context(tc.psum_pool(name="psum", bufs=1))

        def held(shape, dtype, name, tag=None):
            return keep.tile(shape, dtype, name=name, tag=tag or name, align_bytes=64)

        def by_vector(shape, dtype, name):
            return keep.tile(shape, dtype, name=name, tag="by_vector", bufs=34, align_bytes=64)

        def by_scalar(shape, dtype, name):
            return keep.tile(shape, dtype, name=name, tag="by_scalar", bufs=7, align_bytes=64)

        def by_vector_wide(shape, dtype, name):
            return held(shape, dtype, name)

        offs_t = held([P, S // 16], U16, "offs_t")
        offs2_t = held([P, S // 16], U16, "offs2_t")
        sc_win = held([P, T], U8, "sc_win")
        sc2_win = held([P, T], U8, "sc2_win")
        w2s_raw = held([P, H], U8, "w2s_raw")
        w2_raw = held([P, 2 * H], U8, "w2_raw")
        wr = held([P, 2, N], U32, "wr")
        wrs = held([P, 2, N], U8, "wrs")
        rows = held([P, 2 * P], F32, "rows")
        ident = held([P, P], F32, "ident")
        trim_t = held([P, 4], F32, "trim_t")
        low_pat = held([P, 2, 4 * QUART], BF16, "low_pat")
        win, w1raw, w3raw, w1q, w3q, v, v2, allow, least, clipped, hq, ybank, one = ({} for i in range(13))

        def clear(eng, tile):
            eng.memset(tile.bitcast(I32), 0)

        def load_sc():
            src = tab_scales.rearrange("a (g e) t -> e g a t", e=2)
            for e in range(2):
                nc.sync.dma_start(sc_win[e:P:8, :].bitcast(I32), src[e].bitcast(I32))

        def load_plane(dst, src, queue=nc.sync, quads=(0, 1, 2, 3)):
            for r in range(4):
                queue.dma_start(dst[r:P:32, :].bitcast(I32), src[r:16:4, :].bitcast(I32))

        def load_wrs():
            for r in range(4):
                nc.sync.dma_start(
                    wrs[r:P:32, :, :].bitcast(I32),
                    wr_scales[:, r:16:4, :].rearrange("a r n -> r a n").bitcast(I32),
                )

        def load_wr():
            nc.sync.dma_start(wr[:].bitcast(I32), wr_words.rearrange("a p n i -> p a (n i)").bitcast(I32))

        def load_w2():
            nc.sync.dma_start(w2_raw[:].bitcast(I32), w2_words[0].bitcast(I32))

        def load_words(src, name):
            win[name] = held([P, T], U32, name)
            nc.sync.dma_start(win[name][:].bitcast(I32), src.rearrange("p t i -> p (t i)").bitcast(I32))

        def load_w1(a, g):
            w1raw[a, g] = held([P, 4, PASS], F32, "w1raw%d%d" % (a, g))
            src = w1[PASS * a : PASS * (a + 1), PASS * g : PASS * (g + 1)]
            nc.sync.dma_start(w1raw[a, g][:], src.rearrange("(p j) c -> p j c", j=4))

        def load_w3(g, tag):
            w3raw[g] = held([P, 4, N], F32, "w3raw%d" % g, tag)
            src = w3[PASS * g : PASS * (g + 1), :].rearrange("(b t i) n -> t b i n", t=4, i=8)
            for t in range(4):
                nc.sync.dma_start(w3raw[g][:, t, :], src[t])

        def load_rows():
            for r, vec in ((0, slack), (4, low)):
                nc.scalar.dma_start(
                    rows[r : r + 4, :].rearrange("t (b i) -> t b i", i=8),
                    vec.rearrange("(b t i) -> t b i", t=4, i=8),
                )

        def load_trim():
            with nc.allow_non_contiguous_dma(reason="one value of trim for each partition"):
                nc.sync.dma_start(trim_t[:], trim.rearrange("(q p) -> p q", p=P))

        def turn_rows():
            turned = psum.tile([P, 4, P], F32, name="turned", tag="y", bufs=5)
            for g in range(2):
                nc.tensor.transpose(turned[:, g, :], rows[:, P * g : P * (g + 1)], ident[:])
            one["consts"] = held([P, 2, 8], F32, "consts", "w1raw00")
            nc.scalar.copy(one["consts"][:], turned[:, 0:2, 0:8])
            for g in range(2):
                nc.scalar.copy(
                    low_pat[:, g, :].rearrange("p (n t) -> p n t", t=4),
                    one["consts"][:, g, 4:8].unsqueeze(1).to_broadcast([P, QUART, 4]),
                )

        def gather_sc():
            one["sc_got"] = by_vector([P, S], U8, "sc_got")
            nc.vector.tensor_copy(one["sc_got"][:], sc_win[:].indirect(offs_t[:]))

        def copy_sc():
            one["v_sc"] = held([P, S], U8, "v_sc")
            nc.vector.tensor_copy(one["v_sc"][:].bitcast(I32), one["sc_got"][:].bitcast(I32))

        def move_sc():
            for a in range(2):
                for e in range(2):
                    nc.sync.dma_start(
                        one["v_sc"][8 * a + 2 + e : P : 32, :].bitcast(I32),
                        one["sc_got"][16 + 8 * a + e : P : 32, :].bitcast(I32),
                    )

        def gather_sc2():
            one["v2_sc"] = by_vector([P, S], U8, "v2_sc")
            nc.vector.tensor_copy(one["v2_sc"][:], sc2_win[:].indirect(offs2_t[:]))

        def gather_words(name, lst, h):
            got = by_vector([P, HALF], U32, "got_%s_%d" % (name, h))
            cols = slice(HALF // 16 * h, HALF // 16 * (h + 1))
            nc.vector.tensor_copy(got[:], win[name][:].indirect(lst[:, cols]))
            return got

        def gather_v(a, h):
            v[a, h] = gather_words("tab%d" % a, offs_t, h)

        def gather_v2(h):
            v2[h] = gather_words("tab2", offs2_t, h)

        def order_w2():
            one["w2"] = by_vector([P, 2 * H], U8, "w2")
            nc.vector.tensor_copy(
                one["w2"][:].bitcast(I32).rearrange("p (g t b q) -> p g t b q", g=2, t=4, q=4),
                w2_raw[:].bitcast(I32).rearrange("p (g b t q) -> p g t b q", g=2, t=4, q=4),
            )
            one["w2s"] = by_vector([P, H], U8, "w2s")
            nc.vector.tensor_copy(
                one["w2s"][:].bitcast(I32).rearrange("p (g t b q) -> p g t b q", g=2, t=4, q=2),
                w2s_raw[:].bitcast(I32).rearrange("p (g b t q) -> p g t b q", g=2, t=4, q=2),
            )

        def quantise(values, width, name):
            codes = by_vector([P, width], U32, name + "_c")
            scales = held([P, width], U8, name + "_s")
            nc.vector.quantize_mx(out=codes[:].bitcast(FP8X4), scales=scales[:], in_=values)
            return codes, scales

        def cast_w1(a, g, on_vector=False):
            make, move = (by_vector_wide, nc.vector.tensor_copy) if on_vector else (by_scalar, nc.scalar.copy)
            grouped = make([P, 4, P, 4], BF16, "w1g%d%d" % (a, g))
            src = w1raw[a, g][:].rearrange("p j (b t h i) -> p t b h j i", t=4, h=4, i=2)
            for t in range(4):
                move(grouped[:, t, :, :].rearrange("p (b h i) j -> p b h j i", h=4, i=2), src[:, t])
            one["w1g", a, g] = grouped

        def quant_w1(a, g):
            w1q[a, g] = quantise(one["w1g", a, g][:].rearrange("p t m j -> p (t m j)"), PASS, "w1q%d%d" % (a, g))

        def cast_w3(g):
            grouped = by_scalar([P, N, 4], BF16, "w3g%d" % g)
            nc.scalar.copy(
                grouped[:].rearrange("p (c i) t -> p c t i", i=2),
                w3raw[g][:].rearrange("p t (c i) -> p c t i", i=2),
            )
            one["w3g", g] = grouped

        def quant_w3(g):
            w3q[g] = quantise(one["w3g", g][:].rearrange("p n t -> p (n t)"), N, "w3q%d" % g)

        def booked(h, g):
            allow[h, g] = by_scalar([P, 4, HALF], F32, "allow%d%d" % (h, g))
            for t in range(4):
                bank = psum.tile([P, HALF], F32, name="b%d%d" % (h, g), tag="y", bufs=5)
                c0 = PASS * g + P * t
                nc.tensor.matmul_mx(
                    out=bank[:],
                    lhsT=one["w2"][:, 2 * c0 : 2 * (c0 + P)].bitcast(FP4X4),
                    lhsT_scale=one["w2s"][:, c0 : c0 + P],
                    rhs=v2[h][:].bitcast(FP8X4),
                    rhs_scale=one["v2_sc"][:, HALF * h : HALF * (h + 1)],
                    start=True,
                    stop=True,
                )
                nc.scalar.activation(allow[h, g][:, t, :], bank[:], IDENT, bias=one["consts"][:, g, t : t + 1])

        def unit(jq, g, u):
            h, j0 = divmod(QUART * jq, HALF)
            if u == 0:
                least[jq, g] = by_vector([P, 2, QUART, 2], BF16, "least%d%d" % (jq, g))
            bank = psum.tile([P, 2, QUART], F32, name="a%d%d" % (jq, g), tag="a", bufs=3)
            for e in range(2):
                t = 2 * u + e
                for a in (1, 0):
                    codes, scales = w1q[a, g]
                    nc.tensor.matmul_mx(
                        out=bank[:, e, :],
                        lhsT=codes[:, P * t : P * (t + 1)].bitcast(FP8X4),
                        lhsT_scale=scales[:, P * t : P * (t + 1)],
                        rhs=v[a, h][:, j0 : j0 + QUART].bitcast(FP8X4),
                        rhs_scale=one["v_sc"][8 * a : P, QUART * jq : QUART * (jq + 1)],
                        start=(a == 1),
                        stop=(a == 0),
                    )
            nc.vector.tensor_tensor(
                least[jq, g][:, u, :, :].rearrange("p (c i) e -> p c e i", i=4),
                bank[:].rearrange("p e (c i) -> p c e i", i=4),
                allow[h, g][:, 2 * u : 2 * u + 2, j0 : j0 + QUART].rearrange("p e (c i) -> p c e i", i=4),
                ALU.min,
            )

        def clip(jq, g):
            clipped[jq, g] = by_vector([P, 4 * QUART], BF16, "clip%d%d" % (jq, g))
            nc.vector.tensor_tensor(
                clipped[jq, g][:].rearrange("p (n u e) -> p n u e", u=2, e=2),
                least[jq, g][:].rearrange("p u n e -> p n u e"),
                low_pat[:, g, :].rearrange("p (n u e) -> p n u e", u=2, e=2),
                ALU.max,
            )

        def quant_h(jq, g):
            hq[jq, g] = quantise(clipped[jq, g][:], QUART, "hq%d%d" % (jq, g))

        def y_pass(jq, step, tag="y", bufs=5):
            h, j0 = divmod(QUART * jq, HALF)
            for k in range(2):
                first = (jq, k) not in ybank
                if first:
                    tag, bufs = ("a", 3) if (jq, k) == (3, 1) else (tag, bufs)
                    ybank[jq, k] = psum.tile([P, 2, QUART], F32, name="y%d%d" % (jq, k), tag=tag, bufs=bufs)
                for s in range(2):
                    q = 2 * k + s
                    cols = slice(P * q, P * (q + 1))
                    if step < 2:
                        lhs, lhs_s = wr[:, step, cols], wrs[:, step, cols]
                        rhs = v[step, h][:, j0 : j0 + QUART]
                        rhs_s = one["v_sc"][8 * step : P, QUART * jq : QUART * (jq + 1)]
                    else:
                        lhs, lhs_s = w3q[step - 2][0][:, cols], w3q[step - 2][1][:, cols]
                        rhs, rhs_s = hq[jq, step - 2][0][:], hq[jq, step - 2][1][:]
                    nc.tensor.matmul_mx(
                        out=ybank[jq, k][:, s, :],
                        lhsT=lhs.bitcast(FP8X4),
                        lhsT_scale=lhs_s,
                        rhs=rhs.bitcast(FP8X4),
                        rhs_scale=rhs_s,
                        start=(first and s == 0),
                        stop=(step == 3 and s == 1),
                    )

        def y_out(jq, k, on_vector=False):
            if on_vector:
                res = by_vector([P, 2, QUART], F32, "res%d%d" % (jq, k))
            else:
                res = keep.tile([P, 2, QUART], F32, name="res%d%d" % (jq, k), tag="res", bufs=4, align_bytes=64)
            for s in range(2):
                bias = trim_t[:, 2 * k + s : 2 * k + s + 1]
                if on_vector:
                    nc.vector.tensor_scalar(res[:, s, :], ybank[jq, k][:, s, :], bias, None, ALU.add)
                else:
                    nc.scalar.activation(res[:, s, :], ybank[jq, k][:, s, :], IDENT, bias=bias)
            dst = out[2 * P * k : 2 * P * (k + 1), QUART * jq : QUART * (jq + 1)]
            nc.sync.dma_start(dst.rearrange("(s p) n -> p s n", p=P), res[:])

        clear(nc.gpsimd, sc_win[:])
        nc.vector.memset(rows[:], 0.0)
        clear(nc.vector, sc2_win[:])
        clear(nc.vector, w2s_raw[:])
        clear(nc.vector, wrs[:].rearrange("p a n -> p (a n)"))
        load_rows()
        make_identity(nc, ident[:])
        nc.sync.dma_start(offs_t[:], offs)
        load_sc()
        nc.sync.dma_start(offs2_t[:], offs2)
        load_w1(0, 0)
        load_plane(sc2_win, tab2_scales[0])
        load_words(tab2_words[0], "tab2")
        load_w2()
        load_plane(w2s_raw, w2_scales[0])
        load_w1(1, 0)
        load_words(tab_words[0], "tab0")
        gather_sc()
        copy_sc()
        move_sc()
        load_words(tab_words[1], "tab1")
        load_w1(0, 1)
        load_wr()
        load_wrs()
        load_w1(1, 1)
        load_w3(0, "tab2")
        load_w3(1, "tab0")
        load_trim()
        gather_sc2()
        gather_v2(0)
        order_w2()
        cast_w1(0, 0)
        turn_rows()
        booked(0, 0)
        gather_v2(1)
        booked(1, 0)
        cast_w1(1, 0, True)
        quant_w1(0, 0)
        quant_w1(1, 0)
        booked(0, 1)
        booked(1, 1)
        gather_v(0, 0)
        gather_v(0, 1)
        gather_v(1, 0)
        gather_v(1, 1)
        cast_w1(0, 1)
        cast_w1(1, 1)
        cast_w3(0)
        cast_w3(1)
        unit(0, 0, 0)
        unit(0, 0, 1)
        unit(1, 0, 0)
        clip(0,0)
        unit(1, 0, 1)
        quant_h(0,0)
        unit(2, 0, 0)
        clip(1,0)
        unit(2, 0, 1)
        quant_h(1,0)
        quant_w1(0, 1)
        unit(3, 0, 0)
        clip(2,0)
        quant_w1(1, 1)
        unit(3, 0, 1)
        quant_h(2,0)
        y_pass(0, 0)
        y_pass(0, 1)
        y_pass(1, 0)
        y_pass(1, 1)
        clip(3,0)
        unit(0, 1, 0)
        quant_h(3,0)
        quant_w3(0)
        unit(0, 1, 1)
        y_pass(2, 0)
        y_pass(2, 1)
        y_pass(0, 2)
        y_pass(1, 2)
        unit(1, 1, 0)
        clip(0,1)
        quant_w3(1)
        unit(1, 1, 1)
        quant_h(0,1)
        y_pass(0, 3)
        y_out(0, 0)
        y_out(0, 1)
        y_pass(2, 2)
        unit(2, 1, 0)
        clip(1,1)
        unit(2, 1, 1)
        quant_h(1,1)
        y_pass(1, 3)
        y_out(1, 0)
        y_out(1, 1)
        unit(3, 1, 0)
        clip(2,1)
        unit(3, 1, 1)
        quant_h(2,1)
        y_pass(2, 3)
        y_pass(3, 0)
        y_pass(3, 1)
        y_pass(3, 2)
        y_out(2, 0)
        clip(3,1)
        quant_h(3,1)
        y_out(2, 1, True)
        y_pass(3, 3)
        y_out(3, 0)
        y_out(3, 1, True)
